import numpy as np
import ml_dtypes


def mxq(x, axis, fmt="e4m3"):
    dtype, down = {"e4m3": (ml_dtypes.float8_e4m3fn, 7), "e5m2": (ml_dtypes.float8_e5m2, 14)}[fmt]
    v = np.moveaxis(np.asarray(x, np.float32).astype(ml_dtypes.bfloat16).astype(np.float64), axis, -1)
    blocks = v.reshape(v.shape[:-1] + (-1, 32))
    amax = np.abs(blocks).max(-1, keepdims=True)
    byte = np.maximum(np.where(amax > 0, np.frexp(amax)[1] - 1 + 127, 0) - down, 1)
    scale = np.exp2(byte - 127.0)
    codes = (blocks / scale).astype(np.float32).astype(dtype).astype(np.float64)
    return np.moveaxis((codes * scale).reshape(v.shape), -1, axis)


WIDE = False


def mx_kscale(k):
    if not WIDE:
        return np.ones(k)
    levels = np.array([10, -10, 5, -5, 0])
    if k % 512:
        return np.exp2(np.random.permutation(np.resize(levels, k // 32))).repeat(32)
    a = np.empty((k // 512, 16))
    for p in range(k // 512):
        a[p, :8] = np.random.permutation(np.resize(levels, 8))
        for g in range(8):
            far = levels[np.abs(levels - a[p, g]) >= 10]
            a[p, g + 8] = far[np.random.randint(len(far))]
    return np.exp2(a.ravel()).repeat(32)


def f64(x):
    return np.asarray(x).astype(np.float64)


def striped(idx):
    return np.tile(idx.reshape(-1, 16).T, (8, 1)).astype(np.uint16)


def unstriped(offs):
    return offs[:16].T.reshape(-1).astype(np.int64)


def striped8(idx):
    return np.concatenate([x.reshape(-1, 16).T for x in idx]).astype(np.uint16)


def runs(offs, k):
    lists = np.stack([offs[16 * r : 16 * r + 16].T.reshape(-1) for r in range(8)]).astype(np.int64)
    return lists[np.arange(k) % 512 // 64]


def pack_weight(w):
    k, n = w.shape
    w = f64(np.asarray(w, np.float32).astype(ml_dtypes.bfloat16)).reshape(k // 32, 32, n)
    amax = np.abs(w).max(1)
    byte = np.clip(np.where(amax > 0, np.frexp(amax)[1] - 1 + 127 - 7, 1), 1, 254)
    scaled = (w * np.exp2(127.0 - byte)[:, None, :]).reshape(k, n).astype(np.float32)
    words = np.ascontiguousarray(scaled.reshape(k // 512, 128, 4, n).transpose(0, 1, 3, 2)).astype(ml_dtypes.float8_e4m3fn).view(np.uint8)
    return words, np.ascontiguousarray(byte.astype(np.uint8).reshape(k // 512, 16, n))


def unpack_weight(words, scales):
    g, p, n, _ = words.shape
    vals = np.ascontiguousarray(words).view(ml_dtypes.float8_e4m3fn).astype(np.float64) * np.repeat(np.exp2(scales.astype(np.float64) - 127.0), 8, axis=1)[..., None]
    return vals.transpose(0, 1, 3, 2).reshape(g * 512, n)


E2M1 = np.array([0.0, 0.5, 1.0, 1.5, 2.0, 3.0, 4.0, 6.0, -0.0, -0.5, -1.0, -1.5, -2.0, -3.0, -4.0, -6.0])


def pack_fp4(w):
    k, n = w.shape
    w = f64(np.asarray(w, np.float32).astype(ml_dtypes.bfloat16)).reshape(k // 32, 32, n)
    amax = np.abs(w).max(1)
    mant, ex = np.frexp(amax / 6.0)
    byte = np.clip(np.where(amax > 0, np.where(mant > 0.5, ex, ex - 1) + 127, 1), 1, 254)
    scaled = (w * np.exp2(127.0 - byte)[:, None, :]).reshape(k, n).astype(np.float32)
    c = np.ascontiguousarray(scaled.reshape(k // 512, 128, 4, n).transpose(0, 1, 3, 2)).astype(ml_dtypes.float4_e2m1fn).view(np.uint8) & 0xF
    words = (c[..., 0::2] | (c[..., 1::2] << 4)).reshape(k // 512, 128, 2 * n)
    return np.ascontiguousarray(words), np.ascontiguousarray(byte.astype(np.uint8).reshape(k // 512, 16, n))


def unpack_fp4(words, scales):
    g, _, n = scales.shape
    words = np.ascontiguousarray(words).reshape(g, 128, n, 2)
    nib = np.empty((g, 128, n, 4), np.uint8)
    nib[..., 0::2] = words & 0xF
    nib[..., 1::2] = words >> 4
    vals = E2M1[nib] * np.repeat(np.exp2(scales.astype(np.float64) - 127.0), 8, axis=1)[..., None]
    return vals.transpose(0, 1, 3, 2).reshape(g * 512, n)


def planes(y):
    n, m = y.shape
    v = y.astype(np.float32).astype(ml_dtypes.bfloat16).astype(np.float64).reshape(n // 32, 32, m)
    top = np.abs(v).max(1)
    byte = np.clip(np.where(top > 0, np.frexp(top)[1] - 1 + 127 - 7, 1), 1, 254)
    codes = (v * np.exp2(127.0 - byte)[:, None, :]).reshape(n, m).astype(np.float32).astype(ml_dtypes.float8_e4m3fn).view(np.uint8)
    words = codes.reshape(n // 512, 128, 4, m).transpose(0, 1, 3, 2)
    return np.ascontiguousarray(words), np.ascontiguousarray(byte.astype(np.uint8).reshape(n // 512, 16, m))


K, T, S, V, N, H = 512, 2048, 1024, 512, 512, 512


def setup_inputs():
    n = np.random.standard_normal
    s = mx_kscale(K)[:, None]
    u = mx_kscale(H)
    packed_xT = pack_weight(n((K, T)) * s)
    packed_w1 = pack_fp4(n((K, H)) / np.sqrt(K) / s)
    packed_w2 = pack_fp4(n((H, H)) / np.sqrt(2 * H) / u[:, None])
    packed_w3 = pack_fp4(n((H, H)) / np.sqrt(2 * H) / u[:, None])
    packed_w4 = pack_fp4(n((H, N)) / np.sqrt(H) / u[:, None])
    return {
        "x_words": packed_xT[0],
        "x_scales": packed_xT[1],
        "w1_words": packed_w1[0],
        "w1_scales": packed_w1[1],
        "gn": (np.random.uniform(0.5, 1.5, (H, 1)) * u[:, None]).astype(np.float32),
        "w2_words": packed_w2[0],
        "w2_scales": packed_w2[1],
        "w3_words": packed_w3[0],
        "w3_scales": packed_w3[1],
        "res": (2 * n((N, V))).astype(np.float32),
        "w4_words": packed_w4[0],
        "w4_scales": packed_w4[1],
        "offs": striped(np.random.permutation(T)[:S]),
        "lc": striped8(np.stack([np.random.permutation(S)[:V] for _ in range(8)])),
        "rc": striped8(np.stack([np.random.permutation(S)[:V] for _ in range(8)])),
    }


def reference(x_words, x_scales, w1_words, w1_scales, gn, w2_words, w2_scales, w3_words, w3_scales, res, w4_words, w4_scales, offs, lc, rc):
    xq = unpack_weight(x_words, x_scales)[:, unstriped(offs)]
    h = np.tanh(unpack_fp4(w1_words, w1_scales).T @ xq)
    zl = f64(gn) * (h[np.arange(H)[:, None], runs(lc, H)])
    zr = f64(gn) * (h[np.arange(H)[:, None], runs(rc, H)])
    p = np.tanh(unpack_fp4(w2_words, w2_scales).T @ mxq(zl, 0, "e4m3") + unpack_fp4(w3_words, w3_scales).T @ mxq(zr, 0, "e4m3"))
    z = f64(gn) * p
    out_0 = f64(res) + (unpack_fp4(w4_words, w4_scales).T @ mxq(z, 0, "e4m3"))
    return (out_0,) + planes(out_0)

@@ -1,0 +1,244 @@
+from contextlib import ExitStack
+
+import concourse.mybir as mybir
+
+K, T, S, V, N, H = 512, 2048, 1024, 512, 512, 512
+FLOPS = 2 * K * H * S + 2 * 2 * H * H * V + 2 * H * N * V
+
+F32 = mybir.dt.float32
+BF16 = mybir.dt.bfloat16
+I32 = mybir.dt.int32
+U32 = mybir.dt.uint32
+U16 = mybir.dt.uint16
+U8 = mybir.dt.uint8
+FP8X4 = mybir.dt.float8_e4m3fn_x4
+FP4X4 = mybir.dt.float4_e2m1fn_x4
+TANH = mybir.ActivationFunctionType.Tanh
+COPY = mybir.ActivationFunctionType.Copy
+MULT = mybir.AluOpType.mult
+ADD = mybir.AluOpType.add
+
+P = 128
+PACK = 4
+LEAVES = 512
+CHUNK = 256
+BLOCK = 128
+PER_COL = 16
+ON_SCALAR = ((0, 0), (0, 1), (0, 2), (0, 3))
+
+
+def tile_picked_recnn_tanh_po_kernel(
+    tc, x_words, x_scales, w1_words, w1_scales, gn, w2_words, w2_scales, w3_words, w3_scales,
+    res, w4_words, w4_scales, offs, lc, rc, out_0, out_1, out_2,
+):
+    nc = tc.nc
+
+    with ExitStack() as ctx:
+        lists = ctx.enter_context(tc.tile_pool(name="lists", bufs=1))
+        keep = ctx.enter_context(tc.tile_pool(name="keep", bufs=1))
+        ring = ctx.enter_context(tc.tile_pool(name="ring", bufs=4))
+        psum = ctx.enter_context(tc.psum_pool(name="psum", bufs=8))
+
+        def load_scale_rows(queues, plane, scales):
+            for q in range(4):
+                queues[q].dma_start(out=plane[32 * q : 32 * q + 4, :].bitcast(I32), in_=scales[0, 4 * q : 4 * q + 4, :].bitcast(I32))
+
+        def deal(raw_words, raw_scales, name, tag):
+            words = keep.tile([P, 2 * H], U8, name=name + "_words", tag=tag, align_bytes=64)
+            scales = keep.tile([P, H], U8, name=name + "_scales", align_bytes=64)
+            nc.vector.tensor_copy(
+                out=words[:].rearrange("p (t m b) -> p t m b", t=PACK, b=2),
+                in_=raw_words.rearrange("p (m t b) -> p t m b", t=PACK, b=2),
+            )
+            nc.vector.tensor_copy(
+                out=scales[:].rearrange("p (t m) -> p t m", t=PACK),
+                in_=raw_scales.rearrange("p (m t) -> p t m", t=PACK),
+            )
+            return words, scales
+
+        def product(out, weight, t, codes, scales, start, stop):
+            words, bytes_of = weight
+            nc.tensor.matmul_mx(
+                out=out,
+                lhsT=words[:, 2 * P * t : 2 * P * (t + 1)].bitcast(FP4X4),
+                lhsT_scale=bytes_of[:, P * t : P * (t + 1)],
+                rhs=codes.bitcast(FP8X4),
+                rhs_scale=scales,
+                start=start,
+                stop=stop,
+            )
+
+        def interleave(out, planes, copy=nc.scalar.copy):
+            copy(
+                out=out.rearrange("p (c i) t -> p c t i", i=4),
+                in_=planes.rearrange("p t (c i) -> p c t i", i=4),
+            )
+
+        offs_sb = lists.tile([P, S // PER_COL], U16, name="offs_sb")
+        lc_sb = lists.tile([P, V // PER_COL], U16, name="lc_sb")
+        rc_sb = lists.tile([P, V // PER_COL], U16, name="rc_sb")
+        xs = keep.tile([P, T], U8, name="xs", align_bytes=64)
+        xw = keep.tile([P, T], U32, name="xw", align_bytes=64)
+        raw_words = [keep.tile([P, 2 * H], U8, name="raw_words%d" % j, tag="raw_words%d" % j, align_bytes=64) for j in range(4)]
+        raw_scales = keep.tile([P, 4 * H], U8, name="raw_scales", align_bytes=64)
+        gain = keep.tile([P, PACK], F32, name="gain")
+        res_sb = keep.tile([P, PACK, V], F32, name="res_sb", align_bytes=64)
+        sync4 = [nc.sync] * 4
+
+        def load_words(j, words):
+            nc.sync.dma_start(out=raw_words[j][:].bitcast(I32), in_=words[0].bitcast(I32))
+
+        def load_scales(j, scales):
+            load_scale_rows(sync4, raw_scales[:, H * j : H * (j + 1)], scales)
+
+        nc.vector.memset(xs[:].bitcast(I32), 0)
+        nc.vector.memset(raw_scales[:].bitcast(I32), 0)
+        nc.gpsimd.dma_start(out=gain[:], in_=gn.rearrange("(p t) o -> p (t o)", t=PACK))
+        nc.sync.dma_start(offs_sb[:], offs)
+        load_scale_rows(sync4, xs, x_scales)
+        nc.sync.dma_start(lc_sb[:], lc)
+        nc.sync.dma_start(rc_sb[:], rc)
+        nc.sync.dma_start(out=xw[:].bitcast(I32), in_=x_words[0].rearrange("p n t -> p (n t)").bitcast(I32))
+        load_words(0, w1_words)
+        load_scales(0, w1_scales)
+        load_words(1, w2_words)
+        load_words(2, w3_words)
+        load_scales(1, w2_scales)
+        load_scales(2, w3_scales)
+        load_words(3, w4_words)
+        load_scales(3, w4_scales)
+        nc.sync.dma_start(out=res_sb[:], in_=res.rearrange("(p t) v -> p t v", t=PACK))
+
+        def weight(j, tag=None):
+            name = "w%d" % (j + 1)
+            return deal(raw_words[j][:], raw_scales[:, H * j : H * (j + 1)], name, tag or name)
+
+        halves = S // LEAVES
+        leaf_words = [keep.tile([P, LEAVES], U32, name="leaf_words0", align_bytes=64)]
+        leaf_scales = [keep.tile([P, LEAVES], U8, name="leaf_scales%d" % a, align_bytes=64) for a in range(halves)]
+        cols = LEAVES // PER_COL
+
+        def pick(a, out, window):
+            nc.vector.tensor_copy(out=out[:], in_=window[:].indirect(offs_sb[:, cols * a : cols * (a + 1)]))
+
+        pick(0, leaf_scales[0], xs)
+        pick(1, leaf_scales[1], xs)
+        pick(0, leaf_words[0], xw)
+        w1 = weight(0)
+        leaf_words.append(keep.tile([P, LEAVES], U32, name="leaf_words1", tag="raw_words0", align_bytes=64))
+        pick(1, leaf_words[1], xw)
+        w2 = weight(1)
+        w3 = weight(2)
+
+        gh = [keep.tile([P, S], F32, name="gh%d" % t, align_bytes=64) for t in range(PACK)]
+
+        def bank():
+            return psum.tile([P, LEAVES], F32, name="bank")
+
+        def project(a, t):
+            acc = bank()
+            product(acc[:], w1, t, leaf_words[a][:], leaf_scales[a][:], True, True)
+            last = a == halves - 1 and t == PACK - 1
+            h = keep.tile([P, LEAVES], F32, name="h%d%d" % (a, t), tag="late_left" if last else "h%d%d" % (a, t), align_bytes=64)
+            nc.scalar.activation(out=h[:], in_=acc[:], func=TANH)
+            scaled = gh[t][:, LEAVES * a : LEAVES * (a + 1)]
+            if (a, t) in ON_SCALAR:
+                nc.scalar.activation(out=scaled, in_=h[:], func=COPY, scale=gain[:, t : t + 1])
+            else:
+                nc.vector.tensor_scalar(out=scaled, in0=h[:], scalar1=gain[:, t : t + 1], scalar2=None, op0=MULT)
+
+        ccols = CHUNK // PER_COL
+
+        def planes(name, tag):
+            return keep.tile([P, PACK, CHUNK], BF16, name=name, tag=tag, align_bytes=64)
+
+        def fetch(out, c, s, t):
+            which = (lc_sb, rc_sb)[s]
+            nc.vector.tensor_copy(out=out[:, t, :], in_=gh[t][:].indirect(which[:, ccols * c : ccols * (c + 1)]))
+
+        left0 = planes("left0", "left0")
+        right0 = planes("right0", "right0")
+        for t in range(PACK):
+            project(0, t)
+            project(1, t)
+            fetch(left0, 0, 0, t)
+            fetch(right0, 0, 1, t)
+
+        y_words = keep.tile([P, V], U32, name="y_words", align_bytes=64)
+        y_scales = keep.tile([P, V], U8, name="y_scales", align_bytes=64)
+        out_rows = out_0.rearrange("(p t) v -> p t v", t=PACK)
+        out_words = out_1[0].rearrange("p v t -> p (v t)").bitcast(I32)
+
+        def quantise(width, source, name, tag, copy=nc.scalar.copy):
+            grouped = keep.tile([P, width, PACK], BF16, name=name + "_grouped", tag=tag, align_bytes=64)
+            interleave(grouped[:], source, copy)
+            codes = keep.tile([P, width], U32, name=name + "_codes", align_bytes=64)
+            scales = keep.tile([P, width], U8, name=name + "_scales", align_bytes=64)
+            nc.vector.quantize_mx(out=codes[:].bitcast(FP8X4), scales=scales[:], in_=grouped[:].rearrange("p v t -> p (v t)"))
+            return codes, scales
+
+        def combine(b, left, right_planes):
+            j = b % (CHUNK // BLOCK)
+            inner = slice(BLOCK * j, BLOCK * (j + 1))
+            right = quantise(BLOCK, right_planes[:, :, inner], "right%d" % b, "late_right" if b == 0 else "grouped%d" % b, nc.vector.tensor_copy if b == 2 else nc.scalar.copy)
+            acc = bank()[:].rearrange("p (t v) -> p t v", t=PACK)
+            for t in range(PACK):
+                product(acc[:, t, :], w2, t, left[0][:, inner], left[1][:, inner], True, False)
+                product(acc[:, t, :], w3, t, right[0][:], right[1][:], False, True)
+            return acc
+
+        def squash(acc):
+            state = ring.tile([P, BLOCK, PACK], F32, name="state", align_bytes=64)
+            nc.scalar.activation(out=state[:], in_=acc.rearrange("p t v -> p v t"), func=TANH)
+            return state
+
+        def output_layer(state):
+            z = ring.tile([P, BLOCK, PACK], BF16, name="z", align_bytes=64)
+            nc.vector.tensor_tensor(out=z[:], in0=state[:], in1=gain[:].unsqueeze(1).to_broadcast([P, BLOCK, PACK]), op=MULT)
+            z_codes = ring.tile([P, BLOCK], U32, name="z_codes", align_bytes=64)
+            z_scales = ring.tile([P, BLOCK], U8, name="z_scales", align_bytes=64)
+            nc.vector.quantize_mx(out=z_codes[:].bitcast(FP8X4), scales=z_scales[:], in_=z[:].rearrange("p v t -> p (v t)"))
+            out_acc = bank()[:].rearrange("p (t v) -> p t v", t=PACK)
+            for t in range(PACK):
+                product(out_acc[:, t, :], w4, t, z_codes[:], z_scales[:], True, True)
+            return out_acc
+
+        def hand_out(b, out_acc):
+            cut = slice(BLOCK * b, BLOCK * (b + 1))
+            y = ring.tile([P, PACK, BLOCK], F32, name="y", align_bytes=64)
+            nc.vector.tensor_tensor(out=y[:], in0=out_acc, in1=res_sb[:, :, cut], op=ADD)
+            nc.sync.dma_start(out=out_rows[:, :, cut], in_=y[:])
+            return y
+
+        def hand_on(b, y):
+            cut = slice(BLOCK * b, BLOCK * (b + 1))
+            y_grouped = ring.tile([P, BLOCK, PACK], BF16, name="y_grouped", align_bytes=64)
+            interleave(y_grouped[:], y[:])
+            nc.vector.quantize_mx(
+                out=y_words[:, cut].bitcast(FP8X4), scales=y_scales[:, cut], in_=y_grouped[:].rearrange("p v t -> p (v t)")
+            )
+            nc.sync.dma_start(out=out_words[:, cut], in_=y_words[:, cut].bitcast(I32))
+
+        zl0 = quantise(CHUNK, left0[:], "zl0", "zl0_grouped")
+        acc0 = combine(0, zl0, right0)
+        acc1 = combine(1, zl0, right0)
+        left1 = planes("left1", "late_left")
+        right1 = planes("right1", "late_right")
+        for t in range(PACK):
+            fetch(left1, 1, 0, t)
+        for t in range(PACK):
+            fetch(right1, 1, 1, t)
+        zl1 = quantise(CHUNK, left1[:], "zl1", "zl1_grouped")
+        states = [squash(acc0), squash(acc1)]
+        acc2 = combine(2, zl1, right1)
+        acc3 = combine(3, zl1, right1)
+        states.extend([squash(acc2), squash(acc3)])
+        w4 = weight(3, "grouped2")
+        out_accs = [output_layer(state) for state in states]
+        ys = [hand_out(b, out_acc) for b, out_acc in enumerate(out_accs)]
+        for b, y in enumerate(ys):
+            hand_on(b, y)
+
+        for q in range(4):
+            queue = (nc.scalar, nc.sync)[q % 2]
+            queue.dma_start(out=out_2[0, 4 * q : 4 * q + 4, :].bitcast(I32), in_=y_scales[32 * q : 32 * q + 4, :].bitcast(I32))

@@ -24,7 +24,10 @@ LEAVES = 512
 CHUNK = 256
 BLOCK = 128
 PER_COL = 16
-ON_SCALAR = ((0, 0), (0, 1), (0, 2), (0, 3))
+ON_SCALAR = ((0, 0), (0, 1), (0, 2), (0, 3), (1, 1), (1, 2), (1, 3))
+AT_XS = 0
+AT_W1 = 5 * H
+AT_XW = AT_W1 + 4 * LEAVES
 
 
 def tile_picked_recnn_tanh_po_kernel(
@@ -36,25 +39,31 @@ def tile_picked_recnn_tanh_po_kernel(
     with ExitStack() as ctx:
         lists = ctx.enter_context(tc.tile_pool(name="lists", bufs=1))
         keep = ctx.enter_context(tc.tile_pool(name="keep", bufs=1))
+        reused = ctx.enter_context(tc.tile_pool(name="reused", bufs=1))
         ring = ctx.enter_context(tc.tile_pool(name="ring", bufs=4))
         psum = ctx.enter_context(tc.psum_pool(name="psum", bufs=8))
 
-        def load_scale_rows(queues, plane, scales):
+        def load_scale_rows(queue, plane, first, scales):
             for q in range(4):
-                queues[q].dma_start(out=plane[32 * q : 32 * q + 4, :].bitcast(I32), in_=scales[0, 4 * q : 4 * q + 4, :].bitcast(I32))
+                rows = plane[32 * q + first : 32 * q + first + 4, :]
+                queue.dma_start(out=rows.bitcast(I32), in_=scales[0, 4 * q : 4 * q + 4, :].bitcast(I32))
 
-        def deal(raw_words, raw_scales, name, tag):
-            words = keep.tile([P, 2 * H], U8, name=name + "_words", tag=tag, align_bytes=64)
-            scales = keep.tile([P, H], U8, name=name + "_scales", align_bytes=64)
+        def words_tile(tag):
+            return keep.tile([P, 2 * H], U8, name="dealt_" + tag, tag=tag, align_bytes=64)
+
+        def deal_words(raw, words):
             nc.vector.tensor_copy(
                 out=words[:].rearrange("p (t m b) -> p t m b", t=PACK, b=2),
-                in_=raw_words.rearrange("p (m t b) -> p t m b", t=PACK, b=2),
+                in_=raw[:].rearrange("p (m t b) -> p t m b", t=PACK, b=2),
             )
+            return words
+
+        def deal_scales(raw, scales):
             nc.vector.tensor_copy(
                 out=scales[:].rearrange("p (t m) -> p t m", t=PACK),
-                in_=raw_scales.rearrange("p (m t) -> p t m", t=PACK),
+                in_=raw[:].rearrange("p (m t) -> p t m", t=PACK),
             )
-            return words, scales
+            return scales
 
         def product(out, weight, t, codes, scales, start, stop):
             words, bytes_of = weight
@@ -77,41 +86,26 @@ def tile_picked_recnn_tanh_po_kernel(
         offs_sb = lists.tile([P, S // PER_COL], U16, name="offs_sb")
         lc_sb = lists.tile([P, V // PER_COL], U16, name="lc_sb")
         rc_sb = lists.tile([P, V // PER_COL], U16, name="rc_sb")
-        xs = keep.tile([P, T], U8, name="xs", align_bytes=64)
-        xw = keep.tile([P, T], U32, name="xw", align_bytes=64)
-        raw_words = [keep.tile([P, 2 * H], U8, name="raw_words%d" % j, tag="raw_words%d" % j, align_bytes=64) for j in range(4)]
-        raw_scales = keep.tile([P, 4 * H], U8, name="raw_scales", align_bytes=64)
+        xs = reused.tile([P, T], U8, name="xs", offset=AT_XS, align_bytes=64)
+        xw = reused.tile([P, T], U32, name="xw", offset=AT_XW, align_bytes=64)
+        w1_rows = reused.tile([P, H], U8, name="w1_rows", offset=AT_W1, align_bytes=64)
+        w1_raw = reused.tile([P, 2 * H], U8, name="w1_raw", offset=AT_W1 + H, align_bytes=64)
+        moved_rows = keep.tile([P, 2 * H], U8, name="moved_rows", align_bytes=64)
         gain = keep.tile([P, PACK], F32, name="gain")
-        res_sb = keep.tile([P, PACK, V], F32, name="res_sb", align_bytes=64)
-        sync4 = [nc.sync] * 4
 
-        def load_words(j, words):
-            nc.sync.dma_start(out=raw_words[j][:].bitcast(I32), in_=words[0].bitcast(I32))
+        def load_words(queue, tile, words):
+            queue.dma_start(out=tile[:].bitcast(I32), in_=words[0].bitcast(I32))
 
-        def load_scales(j, scales):
-            load_scale_rows(sync4, raw_scales[:, H * j : H * (j + 1)], scales)
-
-        nc.vector.memset(xs[:].bitcast(I32), 0)
-        nc.vector.memset(raw_scales[:].bitcast(I32), 0)
-        nc.gpsimd.dma_start(out=gain[:], in_=gn.rearrange("(p t) o -> p (t o)", t=PACK))
+        for plane in (xs, w1_rows, moved_rows):
+            nc.vector.memset(plane[:].bitcast(I32), 0)
         nc.sync.dma_start(offs_sb[:], offs)
-        load_scale_rows(sync4, xs, x_scales)
+        load_scale_rows(nc.sync, xs, 0, x_scales)
         nc.sync.dma_start(lc_sb[:], lc)
         nc.sync.dma_start(rc_sb[:], rc)
         nc.sync.dma_start(out=xw[:].bitcast(I32), in_=x_words[0].rearrange("p n t -> p (n t)").bitcast(I32))
-        load_words(0, w1_words)
-        load_scales(0, w1_scales)
-        load_words(1, w2_words)
-        load_words(2, w3_words)
-        load_scales(1, w2_scales)
-        load_scales(2, w3_scales)
-        load_words(3, w4_words)
-        load_scales(3, w4_scales)
-        nc.sync.dma_start(out=res_sb[:], in_=res.rearrange("(p t) v -> p t v", t=PACK))
-
-        def weight(j, tag=None):
-            name = "w%d" % (j + 1)
-            return deal(raw_words[j][:], raw_scales[:, H * j : H * (j + 1)], name, tag or name)
+        load_words(nc.gpsimd, w1_raw, w1_words)
+        nc.gpsimd.dma_start(out=gain[:], in_=gn.rearrange("(p t) o -> p (t o)", t=PACK))
+        load_scale_rows(nc.sync, w1_rows, 0, w1_scales)
 
         halves = S // LEAVES
         leaf_words = [keep.tile([P, LEAVES], U32, name="leaf_words0", align_bytes=64)]
@@ -124,11 +118,24 @@ def tile_picked_recnn_tanh_po_kernel(
         pick(0, leaf_scales[0], xs)
         pick(1, leaf_scales[1], xs)
         pick(0, leaf_words[0], xw)
-        w1 = weight(0)
-        leaf_words.append(keep.tile([P, LEAVES], U32, name="leaf_words1", tag="raw_words0", align_bytes=64))
+        w1 = (deal_words(w1_raw, words_tile("w1_dealt")), deal_scales(w1_rows, keep.tile([P, H], U8, name="w1_plane", align_bytes=64))[:])
+        leaf_words.append(reused.tile([P, LEAVES], U32, name="leaf_words1", offset=AT_W1, align_bytes=64))
         pick(1, leaf_words[1], xw)
-        w2 = weight(1)
-        w3 = weight(2)
+
+        w2_raw = reused.tile([P, 2 * H], U8, name="w2_raw", offset=AT_XS, align_bytes=64)
+        packed_rows = reused.tile([P, H], U8, name="packed_rows", offset=AT_XS + 2 * H, align_bytes=64)
+        w3_raw = reused.tile([P, 2 * H], U8, name="w3_raw", offset=AT_XS + 3 * H, align_bytes=64)
+        load_words(nc.sync, w2_raw, w2_words)
+        load_words(nc.sync, w3_raw, w3_words)
+        nc.vector.memset(packed_rows[:].bitcast(I32), 0)
+        for j, scales in enumerate((w2_scales, w3_scales, w4_scales)):
+            load_scale_rows(nc.sync, packed_rows, 4 * j, scales)
+        res_sb = reused.tile([P, PACK, V], F32, name="res_sb", offset=AT_XW + 4 * H, align_bytes=64)
+        nc.sync.dma_start(out=res_sb[:], in_=res.rearrange("(p t) v -> p t v", t=PACK))
+        w2_dealt = deal_words(w2_raw, reused.tile([P, 2 * H], U8, name="w2_dealt", offset=AT_XW, align_bytes=64))
+        w3_dealt = deal_words(w3_raw, reused.tile([P, 2 * H], U8, name="w3_dealt", offset=AT_XW + 2 * H, align_bytes=64))
+        w4_raw = reused.tile([P, 2 * H], U8, name="w4_raw", offset=AT_XS, align_bytes=64)
+        load_words(nc.sync, w4_raw, w4_words)
 
         gh = [keep.tile([P, S], F32, name="gh%d" % t, align_bytes=64) for t in range(PACK)]
 
@@ -138,8 +145,7 @@ def tile_picked_recnn_tanh_po_kernel(
         def project(a, t):
             acc = bank()
             product(acc[:], w1, t, leaf_words[a][:], leaf_scales[a][:], True, True)
-            last = a == halves - 1 and t == PACK - 1
-            h = keep.tile([P, LEAVES], F32, name="h%d%d" % (a, t), tag="late_left" if last else "h%d%d" % (a, t), align_bytes=64)
+            h = keep.tile([P, LEAVES], F32, name="h%d%d" % (a, t), tag="h%d%d" % (a, t), align_bytes=64)
             nc.scalar.activation(out=h[:], in_=acc[:], func=TANH)
             scaled = gh[t][:, LEAVES * a : LEAVES * (a + 1)]
             if (a, t) in ON_SCALAR:
@@ -158,11 +164,24 @@ def tile_picked_recnn_tanh_po_kernel(
 
         left0 = planes("left0", "left0")
         right0 = planes("right0", "right0")
+        project(0, 0)
+        project(0, 1)
         for t in range(PACK):
-            project(0, t)
+            if t >= 2:
+                project(0, t)
             project(1, t)
             fetch(left0, 0, 0, t)
             fetch(right0, 0, 1, t)
+            if t == 1:
+                packed_plane = deal_scales(packed_rows, keep.tile([P, H], U8, name="packed_plane", tag="h11", align_bytes=64))
+        for j in (1, 2):
+            for q in range(4):
+                nc.sync.dma_start(
+                    out=moved_rows[32 * q : 32 * q + 4, H * (j - 1) : H * j].bitcast(I32),
+                    in_=packed_plane[32 * q + 4 * j : 32 * q + 4 * j + 4, :].bitcast(I32),
+                )
+        w2 = (w2_dealt, packed_plane[:])
+        w3 = (w3_dealt, moved_rows[:, 0:H])
 
         y_words = keep.tile([P, V], U32, name="y_words", align_bytes=64)
         y_scales = keep.tile([P, V], U8, name="y_scales", align_bytes=64)
@@ -172,7 +191,7 @@ def tile_picked_recnn_tanh_po_kernel(
         def quantise(width, source, name, tag, copy=nc.scalar.copy):
             grouped = keep.tile([P, width, PACK], BF16, name=name + "_grouped", tag=tag, align_bytes=64)
             interleave(grouped[:], source, copy)
-            codes = keep.tile([P, width], U32, name=name + "_codes", align_bytes=64)
+            codes = keep.tile([P, width], U32, name=name + "_codes", tag=name + "_codes", align_bytes=64)
             scales = keep.tile([P, width], U8, name=name + "_scales", align_bytes=64)
             nc.vector.quantize_mx(out=codes[:].bitcast(FP8X4), scales=scales[:], in_=grouped[:].rearrange("p v t -> p (v t)"))
             return codes, scales
@@ -180,7 +199,7 @@ def tile_picked_recnn_tanh_po_kernel(
         def combine(b, left, right_planes):
             j = b % (CHUNK // BLOCK)
             inner = slice(BLOCK * j, BLOCK * (j + 1))
-            right = quantise(BLOCK, right_planes[:, :, inner], "right%d" % b, "late_right" if b == 0 else "grouped%d" % b, nc.vector.tensor_copy if b == 2 else nc.scalar.copy)
+            right = quantise(BLOCK, right_planes[:, :, inner], "right%d" % b, "grouped%d" % b)
             acc = bank()[:].rearrange("p (t v) -> p t v", t=PACK)
             for t in range(PACK):
                 product(acc[:, t, :], w2, t, left[0][:, inner], left[1][:, inner], True, False)
@@ -192,9 +211,12 @@ def tile_picked_recnn_tanh_po_kernel(
             nc.scalar.activation(out=state[:], in_=acc.rearrange("p t v -> p v t"), func=TANH)
             return state
 
-        def output_layer(state):
+        def gained(state):
             z = ring.tile([P, BLOCK, PACK], BF16, name="z", align_bytes=64)
             nc.vector.tensor_tensor(out=z[:], in0=state[:], in1=gain[:].unsqueeze(1).to_broadcast([P, BLOCK, PACK]), op=MULT)
+            return z
+
+        def output_layer(z):
             z_codes = ring.tile([P, BLOCK], U32, name="z_codes", align_bytes=64)
             z_scales = ring.tile([P, BLOCK], U8, name="z_scales", align_bytes=64)
             nc.vector.quantize_mx(out=z_codes[:].bitcast(FP8X4), scales=z_scales[:], in_=z[:].rearrange("p v t -> p (v t)"))
@@ -222,8 +244,8 @@ def tile_picked_recnn_tanh_po_kernel(
         zl0 = quantise(CHUNK, left0[:], "zl0", "zl0_grouped")
         acc0 = combine(0, zl0, right0)
         acc1 = combine(1, zl0, right0)
-        left1 = planes("left1", "late_left")
-        right1 = planes("right1", "late_right")
+        left1 = planes("left1", "left1")
+        right1 = planes("right1", "left0")
         for t in range(PACK):
             fetch(left1, 1, 0, t)
         for t in range(PACK):
@@ -233,8 +255,13 @@ def tile_picked_recnn_tanh_po_kernel(
         acc2 = combine(2, zl1, right1)
         acc3 = combine(3, zl1, right1)
         states.extend([squash(acc2), squash(acc3)])
-        w4 = weight(3, "grouped2")
-        out_accs = [output_layer(state) for state in states]
+        w4 = (deal_words(w4_raw, words_tile("right0_codes")), moved_rows[:, H : 2 * H])
+        zs = [gained(states[0])]
+        out_accs = []
+        for b in range(len(states)):
+            if b + 1 < len(states):
+                zs.append(gained(states[b + 1]))
+            out_accs.append(output_layer(zs[b]))
         ys = [hand_out(b, out_acc) for b, out_acc in enumerate(out_accs)]
         for b, y in enumerate(ys):
             hand_on(b, y)

@@ -24,10 +24,9 @@ LEAVES = 512
 CHUNK = 256
 BLOCK = 128
 PER_COL = 16
-ON_SCALAR = ((0, 0), (0, 1), (0, 2), (0, 3), (1, 1), (1, 2), (1, 3))
+ON_SCALAR = ((0, 2), (1, 2), (0, 3), (1, 3))
 AT_XS = 0
-AT_W1 = 5 * H
-AT_XW = AT_W1 + 4 * LEAVES
+AT_XW = 5 * H
 
 
 def tile_picked_recnn_tanh_po_kernel(
@@ -48,19 +47,16 @@ def tile_picked_recnn_tanh_po_kernel(
                 rows = plane[32 * q + first : 32 * q + first + 4, :]
                 queue.dma_start(out=rows.bitcast(I32), in_=scales[0, 4 * q : 4 * q + 4, :].bitcast(I32))
 
-        def words_tile(tag):
-            return keep.tile([P, 2 * H], U8, name="dealt_" + tag, tag=tag, align_bytes=64)
-
-        def deal_words(raw, words):
+        def deal_words(raw, words, first=0, last=PACK):
             nc.vector.tensor_copy(
-                out=words[:].rearrange("p (t m b) -> p t m b", t=PACK, b=2),
-                in_=raw[:].rearrange("p (m t b) -> p t m b", t=PACK, b=2),
+                out=words[:].rearrange("p (t h m b) -> p h t m b", h=2, m=P // 2, b=2),
+                in_=raw[:].rearrange("p (h m t b) -> p h t m b", h=2, t=PACK, b=2)[:, :, first:last],
             )
             return words
 
         def deal_scales(raw, scales):
             nc.vector.tensor_copy(
-                out=scales[:].rearrange("p (t m) -> p t m", t=PACK),
+                out=scales[:].rearrange("p (t m) -> p t m", m=P),
                 in_=raw[:].rearrange("p (m t) -> p t m", t=PACK),
             )
             return scales
@@ -88,8 +84,8 @@ def tile_picked_recnn_tanh_po_kernel(
         rc_sb = lists.tile([P, V // PER_COL], U16, name="rc_sb")
         xs = reused.tile([P, T], U8, name="xs", offset=AT_XS, align_bytes=64)
         xw = reused.tile([P, T], U32, name="xw", offset=AT_XW, align_bytes=64)
-        w1_rows = reused.tile([P, H], U8, name="w1_rows", offset=AT_W1, align_bytes=64)
-        w1_raw = reused.tile([P, 2 * H], U8, name="w1_raw", offset=AT_W1 + H, align_bytes=64)
+        w1_rows = keep.tile([P, H], U8, name="w1_rows", tag="w1_rows", align_bytes=64)
+        w1_raw = keep.tile([P, 2 * H], U8, name="w1_raw", align_bytes=64)
         moved_rows = keep.tile([P, 2 * H], U8, name="moved_rows", align_bytes=64)
         gain = keep.tile([P, PACK], F32, name="gain")
 
@@ -108,7 +104,7 @@ def tile_picked_recnn_tanh_po_kernel(
         load_scale_rows(nc.sync, w1_rows, 0, w1_scales)
 
         halves = S // LEAVES
-        leaf_words = [keep.tile([P, LEAVES], U32, name="leaf_words0", align_bytes=64)]
+        leaf_words = [keep.tile([P, LEAVES], U32, name="leaf_words%d" % a, align_bytes=64) for a in range(halves)]
         leaf_scales = [keep.tile([P, LEAVES], U8, name="leaf_scales%d" % a, align_bytes=64) for a in range(halves)]
         cols = LEAVES // PER_COL
 
@@ -118,9 +114,12 @@ def tile_picked_recnn_tanh_po_kernel(
         pick(0, leaf_scales[0], xs)
         pick(1, leaf_scales[1], xs)
         pick(0, leaf_words[0], xw)
-        w1 = (deal_words(w1_raw, words_tile("w1_dealt")), deal_scales(w1_rows, keep.tile([P, H], U8, name="w1_plane", align_bytes=64))[:])
-        leaf_words.append(reused.tile([P, LEAVES], U32, name="leaf_words1", offset=AT_W1, align_bytes=64))
+        first_words = deal_words(w1_raw, keep.tile([P, 2 * P], U8, name="first_words", align_bytes=64), 0, 1)
+        w1_plane = deal_scales(w1_rows, keep.tile([P, H], U8, name="w1_plane", align_bytes=64))
         pick(1, leaf_words[1], xw)
+        rest_words = deal_words(w1_raw, keep.tile([P, 6 * P], U8, name="rest_words", tag="w1_rows", align_bytes=64), 1, PACK)
+        w1_first = (first_words, w1_plane[:, 0:P])
+        w1_rest = (rest_words, w1_plane[:, P:H])
 
         w2_raw = reused.tile([P, 2 * H], U8, name="w2_raw", offset=AT_XS, align_bytes=64)
         packed_rows = reused.tile([P, H], U8, name="packed_rows", offset=AT_XS + 2 * H, align_bytes=64)
@@ -130,10 +129,11 @@ def tile_picked_recnn_tanh_po_kernel(
         nc.vector.memset(packed_rows[:].bitcast(I32), 0)
         for j, scales in enumerate((w2_scales, w3_scales, w4_scales)):
             load_scale_rows(nc.sync, packed_rows, 4 * j, scales)
-        res_sb = reused.tile([P, PACK, V], F32, name="res_sb", offset=AT_XW + 4 * H, align_bytes=64)
+        res_sb = reused.tile([P, PACK, V], F32, name="res_sb", offset=AT_XW + 8 * H, align_bytes=64)
         nc.sync.dma_start(out=res_sb[:], in_=res.rearrange("(p t) v -> p t v", t=PACK))
-        w2_dealt = deal_words(w2_raw, reused.tile([P, 2 * H], U8, name="w2_dealt", offset=AT_XW, align_bytes=64))
-        w3_dealt = deal_words(w3_raw, reused.tile([P, 2 * H], U8, name="w3_dealt", offset=AT_XW + 2 * H, align_bytes=64))
+        w2_dealt = deal_words(w2_raw, reused.tile([P, 2 * H], U8, name="w2_dealt", offset=AT_XW + 3 * H, align_bytes=64))
+        w3_dealt = deal_words(w3_raw, reused.tile([P, 2 * H], U8, name="w3_dealt", offset=AT_XW + 5 * H, align_bytes=64))
+        packed_plane = deal_scales(packed_rows, reused.tile([P, H], U8, name="packed_plane", offset=AT_XW + 7 * H, align_bytes=64))
         w4_raw = reused.tile([P, 2 * H], U8, name="w4_raw", offset=AT_XS, align_bytes=64)
         load_words(nc.sync, w4_raw, w4_words)
 
@@ -144,7 +144,7 @@ def tile_picked_recnn_tanh_po_kernel(
 
         def project(a, t):
             acc = bank()
-            product(acc[:], w1, t, leaf_words[a][:], leaf_scales[a][:], True, True)
+            product(acc[:], w1_rest if t else w1_first, max(t - 1, 0), leaf_words[a][:], leaf_scales[a][:], True, True)
             h = keep.tile([P, LEAVES], F32, name="h%d%d" % (a, t), tag="h%d%d" % (a, t), align_bytes=64)
             nc.scalar.activation(out=h[:], in_=acc[:], func=TANH)
             scaled = gh[t][:, LEAVES * a : LEAVES * (a + 1)]
@@ -164,16 +164,11 @@ def tile_picked_recnn_tanh_po_kernel(
 
         left0 = planes("left0", "left0")
         right0 = planes("right0", "right0")
-        project(0, 0)
-        project(0, 1)
         for t in range(PACK):
-            if t >= 2:
-                project(0, t)
+            project(0, t)
             project(1, t)
             fetch(left0, 0, 0, t)
             fetch(right0, 0, 1, t)
-            if t == 1:
-                packed_plane = deal_scales(packed_rows, keep.tile([P, H], U8, name="packed_plane", tag="h11", align_bytes=64))
         for j in (1, 2):
             for q in range(4):
                 nc.sync.dma_start(
@@ -199,7 +194,7 @@ def tile_picked_recnn_tanh_po_kernel(
         def combine(b, left, right_planes):
             j = b % (CHUNK // BLOCK)
             inner = slice(BLOCK * j, BLOCK * (j + 1))
-            right = quantise(BLOCK, right_planes[:, :, inner], "right%d" % b, "grouped%d" % b)
+            right = quantise(BLOCK, right_planes[:, :, inner], "right%d" % b, "grouped%d" % b, nc.vector.tensor_copy if b == 3 else nc.scalar.copy)
             acc = bank()[:].rearrange("p (t v) -> p t v", t=PACK)
             for t in range(PACK):
                 product(acc[:, t, :], w2, t, left[0][:, inner], left[1][:, inner], True, False)
@@ -225,23 +220,29 @@ def tile_picked_recnn_tanh_po_kernel(
                 product(out_acc[:, t, :], w4, t, z_codes[:], z_scales[:], True, True)
             return out_acc
 
+        y_chunks = [keep.tile([P, PACK, CHUNK], F32, name="y%d" % c, align_bytes=64) for c in range(V // CHUNK)]
+
         def hand_out(b, out_acc):
-            cut = slice(BLOCK * b, BLOCK * (b + 1))
-            y = ring.tile([P, PACK, BLOCK], F32, name="y", align_bytes=64)
-            nc.vector.tensor_tensor(out=y[:], in0=out_acc, in1=res_sb[:, :, cut], op=ADD)
-            nc.sync.dma_start(out=out_rows[:, :, cut], in_=y[:])
+            c, j = divmod(b, CHUNK // BLOCK)
+            y = y_chunks[c][:, :, BLOCK * j : BLOCK * (j + 1)]
+            nc.vector.tensor_tensor(out=y, in0=out_acc, in1=res_sb[:, :, BLOCK * b : BLOCK * (b + 1)], op=ADD)
+            if j == CHUNK // BLOCK - 1:
+                nc.sync.dma_start(out=out_rows[:, :, CHUNK * c : CHUNK * (c + 1)], in_=y_chunks[c][:])
             return y
 
         def hand_on(b, y):
+            c, j = divmod(b, CHUNK // BLOCK)
             cut = slice(BLOCK * b, BLOCK * (b + 1))
             y_grouped = ring.tile([P, BLOCK, PACK], BF16, name="y_grouped", align_bytes=64)
-            interleave(y_grouped[:], y[:])
+            interleave(y_grouped[:], y, nc.vector.tensor_copy if b == 3 else nc.scalar.copy)
             nc.vector.quantize_mx(
                 out=y_words[:, cut].bitcast(FP8X4), scales=y_scales[:, cut], in_=y_grouped[:].rearrange("p v t -> p (v t)")
             )
-            nc.sync.dma_start(out=out_words[:, cut], in_=y_words[:, cut].bitcast(I32))
+            if j == CHUNK // BLOCK - 1:
+                wide = slice(CHUNK * c, CHUNK * (c + 1))
+                nc.sync.dma_start(out=out_words[:, wide], in_=y_words[:, wide].bitcast(I32))
 
-        zl0 = quantise(CHUNK, left0[:], "zl0", "zl0_grouped")
+        zl0 = quantise(CHUNK, left0[:], "zl0", "zl0_grouped", nc.vector.tensor_copy)
         acc0 = combine(0, zl0, right0)
         acc1 = combine(1, zl0, right0)
         left1 = planes("left1", "left1")
@@ -255,13 +256,11 @@ def tile_picked_recnn_tanh_po_kernel(
         acc2 = combine(2, zl1, right1)
         acc3 = combine(3, zl1, right1)
         states.extend([squash(acc2), squash(acc3)])
-        w4 = (deal_words(w4_raw, words_tile("right0_codes")), moved_rows[:, H : 2 * H])
-        zs = [gained(states[0])]
+        w4 = (deal_words(w4_raw, keep.tile([P, 2 * H], U8, name="w4_dealt", tag="grouped0", align_bytes=64)), moved_rows[:, H : 2 * H])
         out_accs = []
-        for b in range(len(states)):
-            if b + 1 < len(states):
-                zs.append(gained(states[b + 1]))
-            out_accs.append(output_layer(zs[b]))
+        for pair in (states[:2], states[2:]):
+            zs = [gained(state) for state in pair]
+            out_accs.extend([output_layer(z) for z in zs])
         ys = [hand_out(b, out_acc) for b, out_acc in enumerate(out_accs)]
         for b, y in enumerate(ys):
             hand_on(b, y)

@@ -24,9 +24,7 @@ LEAVES = 512
 CHUNK = 256
 BLOCK = 128
 PER_COL = 16
-ON_SCALAR = ((0, 2), (1, 2), (0, 3), (1, 3))
-AT_XS = 0
-AT_XW = 5 * H
+ON_SCALAR = ((0, 0), (0, 1), (0, 2), (0, 3), (1, 1), (1, 2), (1, 3))
 
 
 def tile_picked_recnn_tanh_po_kernel(
@@ -49,15 +47,15 @@ def tile_picked_recnn_tanh_po_kernel(
 
         def deal_words(raw, words, first=0, last=PACK):
             nc.vector.tensor_copy(
-                out=words[:].rearrange("p (t h m b) -> p h t m b", h=2, m=P // 2, b=2),
-                in_=raw[:].rearrange("p (h m t b) -> p h t m b", h=2, t=PACK, b=2)[:, :, first:last],
+                out=words[:].rearrange("p (t h m b) -> p h t m b", h=16, m=8, b=2),
+                in_=raw[:].rearrange("p (h m t b) -> p h t m b", h=16, t=PACK, b=2)[:, :, first:last],
             )
             return words
 
         def deal_scales(raw, scales):
             nc.vector.tensor_copy(
-                out=scales[:].rearrange("p (t m) -> p t m", m=P),
-                in_=raw[:].rearrange("p (m t) -> p t m", t=PACK),
+                out=scales[:].rearrange("p (t h m) -> p h t m", h=8, m=16),
+                in_=raw[:].rearrange("p (h m t) -> p h t m", h=8, t=PACK),
             )
             return scales
 
@@ -82,29 +80,37 @@ def tile_picked_recnn_tanh_po_kernel(
         offs_sb = lists.tile([P, S // PER_COL], U16, name="offs_sb")
         lc_sb = lists.tile([P, V // PER_COL], U16, name="lc_sb")
         rc_sb = lists.tile([P, V // PER_COL], U16, name="rc_sb")
-        xs = reused.tile([P, T], U8, name="xs", offset=AT_XS, align_bytes=64)
-        xw = reused.tile([P, T], U32, name="xw", offset=AT_XW, align_bytes=64)
+        xs = keep.tile([P, T], U8, name="xs", align_bytes=64)
+        xw = reused.tile([P, T], U32, name="xw", offset=0, align_bytes=64)
         w1_rows = keep.tile([P, H], U8, name="w1_rows", tag="w1_rows", align_bytes=64)
-        w1_raw = keep.tile([P, 2 * H], U8, name="w1_raw", align_bytes=64)
+        packed_rows = keep.tile([P, H], U8, name="packed_rows", align_bytes=64)
         moved_rows = keep.tile([P, 2 * H], U8, name="moved_rows", align_bytes=64)
+        w1_raw, w2_raw, w3_raw, w4_raw = [keep.tile([P, 2 * H], U8, name="raw%d" % j, align_bytes=64) for j in range(4)]
         gain = keep.tile([P, PACK], F32, name="gain")
+        res_sb = keep.tile([P, PACK, V], F32, name="res_sb", align_bytes=64)
 
-        def load_words(queue, tile, words):
-            queue.dma_start(out=tile[:].bitcast(I32), in_=words[0].bitcast(I32))
+        def load_words(tile, words):
+            nc.sync.dma_start(out=tile[:].bitcast(I32), in_=words[0].bitcast(I32))
 
-        for plane in (xs, w1_rows, moved_rows):
+        for plane in (xs, w1_rows, packed_rows, moved_rows):
             nc.vector.memset(plane[:].bitcast(I32), 0)
+        nc.gpsimd.dma_start(out=gain[:], in_=gn.rearrange("(p t) o -> p (t o)", t=PACK))
         nc.sync.dma_start(offs_sb[:], offs)
         load_scale_rows(nc.sync, xs, 0, x_scales)
         nc.sync.dma_start(lc_sb[:], lc)
         nc.sync.dma_start(rc_sb[:], rc)
         nc.sync.dma_start(out=xw[:].bitcast(I32), in_=x_words[0].rearrange("p n t -> p (n t)").bitcast(I32))
-        load_words(nc.gpsimd, w1_raw, w1_words)
-        nc.gpsimd.dma_start(out=gain[:], in_=gn.rearrange("(p t) o -> p (t o)", t=PACK))
+        load_words(w1_raw, w1_words)
         load_scale_rows(nc.sync, w1_rows, 0, w1_scales)
+        load_words(w2_raw, w2_words)
+        load_words(w3_raw, w3_words)
+        for j, scales in enumerate((w2_scales, w3_scales, w4_scales)):
+            load_scale_rows(nc.sync, packed_rows, 4 * j, scales)
+        load_words(w4_raw, w4_words)
+        nc.sync.dma_start(out=res_sb[:], in_=res.rearrange("(p t) v -> p t v", t=PACK))
 
         halves = S // LEAVES
-        leaf_words = [keep.tile([P, LEAVES], U32, name="leaf_words%d" % a, align_bytes=64) for a in range(halves)]
+        leaf_words = [keep.tile([P, LEAVES], U32, name="leaf_words0", align_bytes=64)]
         leaf_scales = [keep.tile([P, LEAVES], U8, name="leaf_scales%d" % a, align_bytes=64) for a in range(halves)]
         cols = LEAVES // PER_COL
 
@@ -116,26 +122,18 @@ def tile_picked_recnn_tanh_po_kernel(
         pick(0, leaf_words[0], xw)
         first_words = deal_words(w1_raw, keep.tile([P, 2 * P], U8, name="first_words", align_bytes=64), 0, 1)
         w1_plane = deal_scales(w1_rows, keep.tile([P, H], U8, name="w1_plane", align_bytes=64))
+        leaf_words.append(keep.tile([P, LEAVES], U32, name="leaf_words1", tag="w1_rows", align_bytes=64))
         pick(1, leaf_words[1], xw)
-        rest_words = deal_words(w1_raw, keep.tile([P, 6 * P], U8, name="rest_words", tag="w1_rows", align_bytes=64), 1, PACK)
+
+        def dealt(name, place):
+            return reused.tile([P, 2 * H], U8, name=name, offset=2 * H * place, align_bytes=64)
+
+        rest_words = deal_words(w1_raw, reused.tile([P, 6 * P], U8, name="rest_words", offset=0, align_bytes=64), 1, PACK)
         w1_first = (first_words, w1_plane[:, 0:P])
         w1_rest = (rest_words, w1_plane[:, P:H])
-
-        w2_raw = reused.tile([P, 2 * H], U8, name="w2_raw", offset=AT_XS, align_bytes=64)
-        packed_rows = reused.tile([P, H], U8, name="packed_rows", offset=AT_XS + 2 * H, align_bytes=64)
-        w3_raw = reused.tile([P, 2 * H], U8, name="w3_raw", offset=AT_XS + 3 * H, align_bytes=64)
-        load_words(nc.sync, w2_raw, w2_words)
-        load_words(nc.sync, w3_raw, w3_words)
-        nc.vector.memset(packed_rows[:].bitcast(I32), 0)
-        for j, scales in enumerate((w2_scales, w3_scales, w4_scales)):
-            load_scale_rows(nc.sync, packed_rows, 4 * j, scales)
-        res_sb = reused.tile([P, PACK, V], F32, name="res_sb", offset=AT_XW + 8 * H, align_bytes=64)
-        nc.sync.dma_start(out=res_sb[:], in_=res.rearrange("(p t) v -> p t v", t=PACK))
-        w2_dealt = deal_words(w2_raw, reused.tile([P, 2 * H], U8, name="w2_dealt", offset=AT_XW + 3 * H, align_bytes=64))
-        w3_dealt = deal_words(w3_raw, reused.tile([P, 2 * H], U8, name="w3_dealt", offset=AT_XW + 5 * H, align_bytes=64))
-        packed_plane = deal_scales(packed_rows, reused.tile([P, H], U8, name="packed_plane", offset=AT_XW + 7 * H, align_bytes=64))
-        w4_raw = reused.tile([P, 2 * H], U8, name="w4_raw", offset=AT_XS, align_bytes=64)
-        load_words(nc.sync, w4_raw, w4_words)
+        w2_dealt = deal_words(w2_raw, dealt("w2_dealt", 1))
+        w3_dealt = deal_words(w3_raw, dealt("w3_dealt", 2))
+        packed_plane = deal_scales(packed_rows, reused.tile([P, H], U8, name="packed_plane", offset=8 * H, align_bytes=64))
 
         gh = [keep.tile([P, S], F32, name="gh%d" % t, align_bytes=64) for t in range(PACK)]
 
@@ -187,14 +185,14 @@ def tile_picked_recnn_tanh_po_kernel(
             grouped = keep.tile([P, width, PACK], BF16, name=name + "_grouped", tag=tag, align_bytes=64)
             interleave(grouped[:], source, copy)
             codes = keep.tile([P, width], U32, name=name + "_codes", tag=name + "_codes", align_bytes=64)
-            scales = keep.tile([P, width], U8, name=name + "_scales", align_bytes=64)
+            scales = keep.tile([P, width], U8, name=name + "_scales", tag=name + "_scales", align_bytes=64)
             nc.vector.quantize_mx(out=codes[:].bitcast(FP8X4), scales=scales[:], in_=grouped[:].rearrange("p v t -> p (v t)"))
             return codes, scales
 
         def combine(b, left, right_planes):
             j = b % (CHUNK // BLOCK)
             inner = slice(BLOCK * j, BLOCK * (j + 1))
-            right = quantise(BLOCK, right_planes[:, :, inner], "right%d" % b, "grouped%d" % b, nc.vector.tensor_copy if b == 3 else nc.scalar.copy)
+            right = quantise(BLOCK, right_planes[:, :, inner], "right%d" % b, ("grouped0", "grouped1", "right0_codes", "right0_scales")[b], nc.vector.tensor_copy if b == 3 else nc.scalar.copy)
             acc = bank()[:].rearrange("p (t v) -> p t v", t=PACK)
             for t in range(PACK):
                 product(acc[:, t, :], w2, t, left[0][:, inner], left[1][:, inner], True, False)
@@ -242,7 +240,7 @@ def tile_picked_recnn_tanh_po_kernel(
                 wide = slice(CHUNK * c, CHUNK * (c + 1))
                 nc.sync.dma_start(out=out_words[:, wide], in_=y_words[:, wide].bitcast(I32))
 
-        zl0 = quantise(CHUNK, left0[:], "zl0", "zl0_grouped", nc.vector.tensor_copy)
+        zl0 = quantise(CHUNK, left0[:], "zl0", "zl0_grouped")
         acc0 = combine(0, zl0, right0)
         acc1 = combine(1, zl0, right0)
         left1 = planes("left1", "left1")
@@ -256,11 +254,13 @@ def tile_picked_recnn_tanh_po_kernel(
         acc2 = combine(2, zl1, right1)
         acc3 = combine(3, zl1, right1)
         states.extend([squash(acc2), squash(acc3)])
-        w4 = (deal_words(w4_raw, keep.tile([P, 2 * H], U8, name="w4_dealt", tag="grouped0", align_bytes=64)), moved_rows[:, H : 2 * H])
+        w4 = (deal_words(w4_raw, dealt("w4_dealt", 3)), moved_rows[:, H : 2 * H])
+        zs = [gained(states[0])]
         out_accs = []
-        for pair in (states[:2], states[2:]):
-            zs = [gained(state) for state in pair]
-            out_accs.extend([output_layer(z) for z in zs])
+        for b in range(len(states)):
+            if b + 1 < len(states):
+                zs.append(gained(states[b + 1]))
+            out_accs.append(output_layer(zs[b]))
         ys = [hand_out(b, out_acc) for b, out_acc in enumerate(out_accs)]
         for b, y in enumerate(ys):
             hand_on(b, y)

@@ -20,11 +20,18 @@ ADD = mybir.AluOpType.add
 
 P = 128
 PACK = 4
+QUADRANTS = 4
+PER_COL = 16
+BANK = 512
 LEAVES = 512
 CHUNK = 256
 BLOCK = 128
-PER_COL = 16
-ON_SCALAR = ((0, 0), (0, 1), (0, 2), (0, 3), (1, 1), (1, 2), (1, 3))
+BLOCKS = V // BLOCK
+PER_CHUNK = CHUNK // BLOCK
+WORD_BYTES = 2 * H
+LINE_WORDS = 8
+LINE_BYTES = 16
+RUN = 4
 
 
 def tile_picked_recnn_tanh_po_kernel(
@@ -37,138 +44,148 @@ def tile_picked_recnn_tanh_po_kernel(
         lists = ctx.enter_context(tc.tile_pool(name="lists", bufs=1))
         keep = ctx.enter_context(tc.tile_pool(name="keep", bufs=1))
         reused = ctx.enter_context(tc.tile_pool(name="reused", bufs=1))
-        ring = ctx.enter_context(tc.tile_pool(name="ring", bufs=4))
+        per_block = ctx.enter_context(tc.tile_pool(name="per_block", bufs=BLOCKS))
         psum = ctx.enter_context(tc.psum_pool(name="psum", bufs=8))
 
-        def load_scale_rows(queue, plane, first, scales):
-            for q in range(4):
-                rows = plane[32 * q + first : 32 * q + first + 4, :]
-                queue.dma_start(out=rows.bitcast(I32), in_=scales[0, 4 * q : 4 * q + 4, :].bitcast(I32))
+        def load_words(tile, words):
+            nc.sync.dma_start(out=tile[:].bitcast(I32), in_=words[0].bitcast(I32))
 
-        def deal_words(raw, words, first=0, last=PACK):
+        def load_scale_rows(tile, first, scales):
+            for q in range(QUADRANTS):
+                rows = tile[32 * q + first : 32 * q + first + 4, :]
+                nc.sync.dma_start(out=rows.bitcast(I32), in_=scales[0, 4 * q : 4 * q + 4, :].bitcast(I32))
+
+        def deal_words(raw, dealt, first=0, last=PACK):
+            steps = P // LINE_WORDS
             nc.vector.tensor_copy(
-                out=words[:].rearrange("p (t h m b) -> p h t m b", h=16, m=8, b=2),
-                in_=raw[:].rearrange("p (h m t b) -> p h t m b", h=16, t=PACK, b=2)[:, :, first:last],
+                out=dealt[:].bitcast(U16).rearrange("p (t s m) -> p s t m", s=steps, m=LINE_WORDS),
+                in_=raw[:].bitcast(U16).rearrange("p (s m t) -> p s t m", s=steps, t=PACK)[:, :, first:last],
             )
-            return words
+            return dealt
 
-        def deal_scales(raw, scales):
+        def deal_scales(raw, dealt):
+            steps = P // LINE_BYTES
             nc.vector.tensor_copy(
-                out=scales[:].rearrange("p (t h m) -> p h t m", h=8, m=16),
-                in_=raw[:].rearrange("p (h m t) -> p h t m", h=8, t=PACK),
+                out=dealt[:].rearrange("p (t s m) -> p s t m", s=steps, m=LINE_BYTES),
+                in_=raw[:].rearrange("p (s m t) -> p s t m", s=steps, t=PACK),
             )
-            return scales
+            return dealt
 
-        def product(out, weight, t, codes, scales, start, stop):
-            words, bytes_of = weight
+        def product(out, weight, place, codes, scales, start, stop):
+            dealt_words, dealt_scales = weight
             nc.tensor.matmul_mx(
                 out=out,
-                lhsT=words[:, 2 * P * t : 2 * P * (t + 1)].bitcast(FP4X4),
-                lhsT_scale=bytes_of[:, P * t : P * (t + 1)],
+                lhsT=dealt_words[:, 2 * P * place : 2 * P * (place + 1)].bitcast(FP4X4),
+                lhsT_scale=dealt_scales[:, P * place : P * (place + 1)],
                 rhs=codes.bitcast(FP8X4),
                 rhs_scale=scales,
                 start=start,
                 stop=stop,
             )
 
-        def interleave(out, planes, copy=nc.scalar.copy):
+        def regroup(b, grouped, tiles):
+            copy = nc.vector.tensor_copy if b == BLOCKS - 1 else nc.scalar.copy
             copy(
-                out=out.rearrange("p (c i) t -> p c t i", i=4),
-                in_=planes.rearrange("p t (c i) -> p c t i", i=4),
+                out=grouped.rearrange("p (c i) t -> p c t i", i=RUN),
+                in_=tiles.rearrange("p t (c i) -> p c t i", i=RUN),
             )
+
+        def quantise(codes, scales, grouped):
+            nc.vector.quantize_mx(out=codes.bitcast(FP8X4), scales=scales, in_=grouped.rearrange("p v t -> p (v t)"))
+
+        def bank():
+            return psum.tile([P, BANK], F32, name="bank")
+
+        def bank_of_tiles():
+            return bank()[:].rearrange("p (t v) -> p t v", t=PACK)
 
         offs_sb = lists.tile([P, S // PER_COL], U16, name="offs_sb")
         lc_sb = lists.tile([P, V // PER_COL], U16, name="lc_sb")
         rc_sb = lists.tile([P, V // PER_COL], U16, name="rc_sb")
-        xs = keep.tile([P, T], U8, name="xs", align_bytes=64)
-        xw = reused.tile([P, T], U32, name="xw", offset=0, align_bytes=64)
+        token_scales = keep.tile([P, T], U8, name="token_scales", align_bytes=64)
+        token_words = reused.tile([P, T], U32, name="token_words", offset=0, align_bytes=64)
         w1_rows = keep.tile([P, H], U8, name="w1_rows", tag="w1_rows", align_bytes=64)
         packed_rows = keep.tile([P, H], U8, name="packed_rows", align_bytes=64)
         moved_rows = keep.tile([P, 2 * H], U8, name="moved_rows", align_bytes=64)
-        w1_raw, w2_raw, w3_raw, w4_raw = [keep.tile([P, 2 * H], U8, name="raw%d" % j, align_bytes=64) for j in range(4)]
+        w1_raw, w2_raw, w3_raw, w4_raw = [
+            keep.tile([P, WORD_BYTES], U8, name="w%d_raw" % j, align_bytes=64) for j in (1, 2, 3, 4)
+        ]
         gain = keep.tile([P, PACK], F32, name="gain")
         res_sb = keep.tile([P, PACK, V], F32, name="res_sb", align_bytes=64)
 
-        def load_words(tile, words):
-            nc.sync.dma_start(out=tile[:].bitcast(I32), in_=words[0].bitcast(I32))
-
-        for plane in (xs, w1_rows, packed_rows, moved_rows):
-            nc.vector.memset(plane[:].bitcast(I32), 0)
+        for tile in (token_scales, w1_rows, packed_rows, moved_rows):
+            nc.vector.memset(tile[:].bitcast(I32), 0)
         nc.gpsimd.dma_start(out=gain[:], in_=gn.rearrange("(p t) o -> p (t o)", t=PACK))
         nc.sync.dma_start(offs_sb[:], offs)
-        load_scale_rows(nc.sync, xs, 0, x_scales)
+        load_scale_rows(token_scales, 0, x_scales)
         nc.sync.dma_start(lc_sb[:], lc)
         nc.sync.dma_start(rc_sb[:], rc)
-        nc.sync.dma_start(out=xw[:].bitcast(I32), in_=x_words[0].rearrange("p n t -> p (n t)").bitcast(I32))
+        nc.sync.dma_start(out=token_words[:].bitcast(I32), in_=x_words[0].rearrange("p n t -> p (n t)").bitcast(I32))
         load_words(w1_raw, w1_words)
-        load_scale_rows(nc.sync, w1_rows, 0, w1_scales)
+        load_scale_rows(w1_rows, 0, w1_scales)
         load_words(w2_raw, w2_words)
         load_words(w3_raw, w3_words)
         for j, scales in enumerate((w2_scales, w3_scales, w4_scales)):
-            load_scale_rows(nc.sync, packed_rows, 4 * j, scales)
+            load_scale_rows(packed_rows, 4 * j, scales)
         load_words(w4_raw, w4_words)
         nc.sync.dma_start(out=res_sb[:], in_=res.rearrange("(p t) v -> p t v", t=PACK))
 
-        halves = S // LEAVES
         leaf_words = [keep.tile([P, LEAVES], U32, name="leaf_words0", align_bytes=64)]
-        leaf_scales = [keep.tile([P, LEAVES], U8, name="leaf_scales%d" % a, align_bytes=64) for a in range(halves)]
-        cols = LEAVES // PER_COL
+        leaf_scales = [keep.tile([P, LEAVES], U8, name="leaf_scales%d" % half, align_bytes=64) for half in range(2)]
 
-        def pick(a, out, window):
-            nc.vector.tensor_copy(out=out[:], in_=window[:].indirect(offs_sb[:, cols * a : cols * (a + 1)]))
+        def pick(half, picked, window):
+            columns = LEAVES // PER_COL
+            entries = offs_sb[:, columns * half : columns * (half + 1)]
+            nc.vector.tensor_copy(out=picked[:], in_=window[:].indirect(entries))
 
-        pick(0, leaf_scales[0], xs)
-        pick(1, leaf_scales[1], xs)
-        pick(0, leaf_words[0], xw)
+        def after_tokens(name, size, place):
+            return reused.tile([P, size], U8, name=name, offset=WORD_BYTES * place, align_bytes=64)
+
+        pick(0, leaf_scales[0], token_scales)
+        pick(1, leaf_scales[1], token_scales)
+        pick(0, leaf_words[0], token_words)
         first_words = deal_words(w1_raw, keep.tile([P, 2 * P], U8, name="first_words", align_bytes=64), 0, 1)
         w1_plane = deal_scales(w1_rows, keep.tile([P, H], U8, name="w1_plane", align_bytes=64))
         leaf_words.append(keep.tile([P, LEAVES], U32, name="leaf_words1", tag="w1_rows", align_bytes=64))
-        pick(1, leaf_words[1], xw)
-
-        def dealt(name, place):
-            return reused.tile([P, 2 * H], U8, name=name, offset=2 * H * place, align_bytes=64)
-
-        rest_words = deal_words(w1_raw, reused.tile([P, 6 * P], U8, name="rest_words", offset=0, align_bytes=64), 1, PACK)
+        pick(1, leaf_words[1], token_words)
+        rest_words = deal_words(w1_raw, after_tokens("rest_words", 2 * P * (PACK - 1), 0), 1, PACK)
         w1_first = (first_words, w1_plane[:, 0:P])
         w1_rest = (rest_words, w1_plane[:, P:H])
-        w2_dealt = deal_words(w2_raw, dealt("w2_dealt", 1))
-        w3_dealt = deal_words(w3_raw, dealt("w3_dealt", 2))
-        packed_plane = deal_scales(packed_rows, reused.tile([P, H], U8, name="packed_plane", offset=8 * H, align_bytes=64))
+        w2_dealt = deal_words(w2_raw, after_tokens("w2_dealt", WORD_BYTES, 1))
+        w3_dealt = deal_words(w3_raw, after_tokens("w3_dealt", WORD_BYTES, 2))
+        packed_plane = deal_scales(packed_rows, after_tokens("packed_plane", H, 4))
 
-        gh = [keep.tile([P, S], F32, name="gh%d" % t, align_bytes=64) for t in range(PACK)]
+        windows = [keep.tile([P, S], F32, name="window%d" % t, align_bytes=64) for t in range(PACK)]
 
-        def bank():
-            return psum.tile([P, LEAVES], F32, name="bank")
-
-        def project(a, t):
+        def project(half, t):
             acc = bank()
-            product(acc[:], w1_rest if t else w1_first, max(t - 1, 0), leaf_words[a][:], leaf_scales[a][:], True, True)
-            h = keep.tile([P, LEAVES], F32, name="h%d%d" % (a, t), tag="h%d%d" % (a, t), align_bytes=64)
+            weight, place = (w1_first, 0) if t == 0 else (w1_rest, t - 1)
+            product(acc[:], weight, place, leaf_words[half][:], leaf_scales[half][:], True, True)
+            h = keep.tile([P, LEAVES], F32, name="h%d%d" % (half, t), align_bytes=64)
             nc.scalar.activation(out=h[:], in_=acc[:], func=TANH)
-            scaled = gh[t][:, LEAVES * a : LEAVES * (a + 1)]
-            if (a, t) in ON_SCALAR:
-                nc.scalar.activation(out=scaled, in_=h[:], func=COPY, scale=gain[:, t : t + 1])
+            gained = windows[t][:, LEAVES * half : LEAVES * (half + 1)]
+            if t == 0:
+                nc.vector.tensor_scalar(out=gained, in0=h[:], scalar1=gain[:, t : t + 1], scalar2=None, op0=MULT)
             else:
-                nc.vector.tensor_scalar(out=scaled, in0=h[:], scalar1=gain[:, t : t + 1], scalar2=None, op0=MULT)
+                nc.scalar.activation(out=gained, in_=h[:], func=COPY, scale=gain[:, t : t + 1])
 
-        ccols = CHUNK // PER_COL
-
-        def planes(name, tag):
+        def children(name, tag):
             return keep.tile([P, PACK, CHUNK], BF16, name=name, tag=tag, align_bytes=64)
 
-        def fetch(out, c, s, t):
-            which = (lc_sb, rc_sb)[s]
-            nc.vector.tensor_copy(out=out[:, t, :], in_=gh[t][:].indirect(which[:, ccols * c : ccols * (c + 1)]))
+        def fetch(fetched, list_sb, c, t):
+            columns = CHUNK // PER_COL
+            entries = list_sb[:, columns * c : columns * (c + 1)]
+            nc.vector.tensor_copy(out=fetched[:, t, :], in_=windows[t][:].indirect(entries))
 
-        left0 = planes("left0", "left0")
-        right0 = planes("right0", "right0")
+        left0 = children("left0", "left0")
+        right0 = children("right0", "right0")
         for t in range(PACK):
             project(0, t)
             project(1, t)
-            fetch(left0, 0, 0, t)
-            fetch(right0, 0, 1, t)
+            fetch(left0, lc_sb, 0, t)
+            fetch(right0, rc_sb, 0, t)
         for j in (1, 2):
-            for q in range(4):
+            for q in range(QUADRANTS):
                 nc.sync.dma_start(
                     out=moved_rows[32 * q : 32 * q + 4, H * (j - 1) : H * j].bitcast(I32),
                     in_=packed_plane[32 * q + 4 * j : 32 * q + 4 * j + 4, :].bitcast(I32),
@@ -178,93 +195,100 @@ def tile_picked_recnn_tanh_po_kernel(
 
         y_words = keep.tile([P, V], U32, name="y_words", align_bytes=64)
         y_scales = keep.tile([P, V], U8, name="y_scales", align_bytes=64)
+        y_chunks = [keep.tile([P, PACK, CHUNK], F32, name="y%d" % c, align_bytes=64) for c in range(V // CHUNK)]
         out_rows = out_0.rearrange("(p t) v -> p t v", t=PACK)
         out_words = out_1[0].rearrange("p v t -> p (v t)").bitcast(I32)
 
-        def quantise(width, source, name, tag, copy=nc.scalar.copy):
-            grouped = keep.tile([P, width, PACK], BF16, name=name + "_grouped", tag=tag, align_bytes=64)
-            interleave(grouped[:], source, copy)
+        def mx_operand(name, width):
             codes = keep.tile([P, width], U32, name=name + "_codes", tag=name + "_codes", align_bytes=64)
             scales = keep.tile([P, width], U8, name=name + "_scales", tag=name + "_scales", align_bytes=64)
-            nc.vector.quantize_mx(out=codes[:].bitcast(FP8X4), scales=scales[:], in_=grouped[:].rearrange("p v t -> p (v t)"))
             return codes, scales
 
-        def combine(b, left, right_planes):
-            j = b % (CHUNK // BLOCK)
-            inner = slice(BLOCK * j, BLOCK * (j + 1))
-            right = quantise(BLOCK, right_planes[:, :, inner], "right%d" % b, ("grouped0", "grouped1", "right0_codes", "right0_scales")[b], nc.vector.tensor_copy if b == 3 else nc.scalar.copy)
-            acc = bank()[:].rearrange("p (t v) -> p t v", t=PACK)
+        def quantise_left(c, fetched):
+            grouped = keep.tile([P, CHUNK, PACK], BF16, name="zl%d_grouped" % c, align_bytes=64)
+            regroup(PER_CHUNK * c, grouped[:], fetched[:])
+            codes, scales = mx_operand("zl%d" % c, CHUNK)
+            quantise(codes[:], scales[:], grouped[:])
+            return codes, scales
+
+        zr_grouped_tags = ("zr0_grouped", "zr1_grouped", "zr0_codes", "zr0_scales")
+
+        def combine(b, zl, fetched):
+            inner = slice(BLOCK * (b % PER_CHUNK), BLOCK * (b % PER_CHUNK + 1))
+            grouped = keep.tile([P, BLOCK, PACK], BF16, name="zr%d_grouped" % b, tag=zr_grouped_tags[b], align_bytes=64)
+            regroup(b, grouped[:], fetched[:, :, inner])
+            codes, scales = mx_operand("zr%d" % b, BLOCK)
+            quantise(codes[:], scales[:], grouped[:])
+            acc = bank_of_tiles()
             for t in range(PACK):
-                product(acc[:, t, :], w2, t, left[0][:, inner], left[1][:, inner], True, False)
-                product(acc[:, t, :], w3, t, right[0][:], right[1][:], False, True)
+                product(acc[:, t, :], w2, t, zl[0][:, inner], zl[1][:, inner], True, False)
+                product(acc[:, t, :], w3, t, codes[:], scales[:], False, True)
             return acc
 
         def squash(acc):
-            state = ring.tile([P, BLOCK, PACK], F32, name="state", align_bytes=64)
+            state = per_block.tile([P, BLOCK, PACK], F32, name="state", align_bytes=64)
             nc.scalar.activation(out=state[:], in_=acc.rearrange("p t v -> p v t"), func=TANH)
             return state
 
-        def gained(state):
-            z = ring.tile([P, BLOCK, PACK], BF16, name="z", align_bytes=64)
-            nc.vector.tensor_tensor(out=z[:], in0=state[:], in1=gain[:].unsqueeze(1).to_broadcast([P, BLOCK, PACK]), op=MULT)
+        def apply_gain(state):
+            z = per_block.tile([P, BLOCK, PACK], BF16, name="z", align_bytes=64)
+            gains = gain[:].unsqueeze(1).to_broadcast([P, BLOCK, PACK])
+            nc.vector.tensor_tensor(out=z[:], in0=state[:], in1=gains, op=MULT)
             return z
 
         def output_layer(z):
-            z_codes = ring.tile([P, BLOCK], U32, name="z_codes", align_bytes=64)
-            z_scales = ring.tile([P, BLOCK], U8, name="z_scales", align_bytes=64)
-            nc.vector.quantize_mx(out=z_codes[:].bitcast(FP8X4), scales=z_scales[:], in_=z[:].rearrange("p v t -> p (v t)"))
-            out_acc = bank()[:].rearrange("p (t v) -> p t v", t=PACK)
+            z_codes = per_block.tile([P, BLOCK], U32, name="z_codes", align_bytes=64)
+            z_scales = per_block.tile([P, BLOCK], U8, name="z_scales", align_bytes=64)
+            quantise(z_codes[:], z_scales[:], z[:])
+            acc = bank_of_tiles()
             for t in range(PACK):
-                product(out_acc[:, t, :], w4, t, z_codes[:], z_scales[:], True, True)
-            return out_acc
+                product(acc[:, t, :], w4, t, z_codes[:], z_scales[:], True, True)
+            return acc
 
-        y_chunks = [keep.tile([P, PACK, CHUNK], F32, name="y%d" % c, align_bytes=64) for c in range(V // CHUNK)]
-
-        def hand_out(b, out_acc):
-            c, j = divmod(b, CHUNK // BLOCK)
+        def add_residual(b, acc):
+            c, j = divmod(b, PER_CHUNK)
             y = y_chunks[c][:, :, BLOCK * j : BLOCK * (j + 1)]
-            nc.vector.tensor_tensor(out=y, in0=out_acc, in1=res_sb[:, :, BLOCK * b : BLOCK * (b + 1)], op=ADD)
-            if j == CHUNK // BLOCK - 1:
+            nc.vector.tensor_tensor(out=y, in0=acc, in1=res_sb[:, :, BLOCK * b : BLOCK * (b + 1)], op=ADD)
+            if j == PER_CHUNK - 1:
                 nc.sync.dma_start(out=out_rows[:, :, CHUNK * c : CHUNK * (c + 1)], in_=y_chunks[c][:])
             return y
 
         def hand_on(b, y):
-            c, j = divmod(b, CHUNK // BLOCK)
-            cut = slice(BLOCK * b, BLOCK * (b + 1))
-            y_grouped = ring.tile([P, BLOCK, PACK], BF16, name="y_grouped", align_bytes=64)
-            interleave(y_grouped[:], y, nc.vector.tensor_copy if b == 3 else nc.scalar.copy)
-            nc.vector.quantize_mx(
-                out=y_words[:, cut].bitcast(FP8X4), scales=y_scales[:, cut], in_=y_grouped[:].rearrange("p v t -> p (v t)")
-            )
-            if j == CHUNK // BLOCK - 1:
-                wide = slice(CHUNK * c, CHUNK * (c + 1))
-                nc.sync.dma_start(out=out_words[:, wide], in_=y_words[:, wide].bitcast(I32))
+            c, j = divmod(b, PER_CHUNK)
+            nodes = slice(BLOCK * b, BLOCK * (b + 1))
+            y_grouped = per_block.tile([P, BLOCK, PACK], BF16, name="y_grouped", align_bytes=64)
+            regroup(b, y_grouped[:], y)
+            quantise(y_words[:, nodes], y_scales[:, nodes], y_grouped[:])
+            if j == PER_CHUNK - 1:
+                chunk = slice(CHUNK * c, CHUNK * (c + 1))
+                nc.sync.dma_start(out=out_words[:, chunk], in_=y_words[:, chunk].bitcast(I32))
 
-        zl0 = quantise(CHUNK, left0[:], "zl0", "zl0_grouped")
-        acc0 = combine(0, zl0, right0)
-        acc1 = combine(1, zl0, right0)
-        left1 = planes("left1", "left1")
-        right1 = planes("right1", "left0")
+        zl0 = quantise_left(0, left0)
+        accs = [combine(b, zl0, right0) for b in range(PER_CHUNK)]
+        left1 = children("left1", "left1")
+        right1 = children("right1", "left0")
         for t in range(PACK):
-            fetch(left1, 1, 0, t)
+            fetch(left1, lc_sb, 1, t)
         for t in range(PACK):
-            fetch(right1, 1, 1, t)
-        zl1 = quantise(CHUNK, left1[:], "zl1", "zl1_grouped")
-        states = [squash(acc0), squash(acc1)]
-        acc2 = combine(2, zl1, right1)
-        acc3 = combine(3, zl1, right1)
-        states.extend([squash(acc2), squash(acc3)])
-        w4 = (deal_words(w4_raw, dealt("w4_dealt", 3)), moved_rows[:, H : 2 * H])
-        zs = [gained(states[0])]
+            fetch(right1, rc_sb, 1, t)
+        zl1 = quantise_left(1, left1)
+        states = [squash(acc) for acc in accs]
+        accs = [combine(b, zl1, right1) for b in range(PER_CHUNK, BLOCKS)]
+        states.extend([squash(acc) for acc in accs])
+        w4 = (deal_words(w4_raw, after_tokens("w4_dealt", WORD_BYTES, 3)), moved_rows[:, H : 2 * H])
+
+        zs = [apply_gain(states[0])]
         out_accs = []
-        for b in range(len(states)):
-            if b + 1 < len(states):
-                zs.append(gained(states[b + 1]))
+        for b in range(BLOCKS):
+            if b + 1 < BLOCKS:
+                zs.append(apply_gain(states[b + 1]))
             out_accs.append(output_layer(zs[b]))
-        ys = [hand_out(b, out_acc) for b, out_acc in enumerate(out_accs)]
+        ys = [add_residual(b, acc) for b, acc in enumerate(out_accs)]
         for b, y in enumerate(ys):
             hand_on(b, y)
 
-        for q in range(4):
+        for q in range(QUADRANTS):
             queue = (nc.scalar, nc.sync)[q % 2]
-            queue.dma_start(out=out_2[0, 4 * q : 4 * q + 4, :].bitcast(I32), in_=y_scales[32 * q : 32 * q + 4, :].bitcast(I32))
+            queue.dma_start(
+                out=out_2[0, 4 * q : 4 * q + 4, :].bitcast(I32), in_=y_scales[32 * q : 32 * q + 4, :].bitcast(I32)
+            )

from contextlib import ExitStack

import concourse.mybir as mybir

K, T, S, V, N, H = 512, 2048, 1024, 512, 512, 512
FLOPS = 2 * K * H * S + 2 * 2 * H * H * V + 2 * H * N * V

F32 = mybir.dt.float32
BF16 = mybir.dt.bfloat16
I32 = mybir.dt.int32
U32 = mybir.dt.uint32
U16 = mybir.dt.uint16
U8 = mybir.dt.uint8
FP8X4 = mybir.dt.float8_e4m3fn_x4
FP4X4 = mybir.dt.float4_e2m1fn_x4
TANH = mybir.ActivationFunctionType.Tanh
COPY = mybir.ActivationFunctionType.Copy
MULT = mybir.AluOpType.mult
ADD = mybir.AluOpType.add

P = 128
PACK = 4
QUADRANTS = 4
PER_COL = 16
BANK = 512
LEAVES = 512
CHUNK = 256
BLOCK = 128
BLOCKS = V // BLOCK
PER_CHUNK = CHUNK // BLOCK
WORD_BYTES = 2 * H
LINE_WORDS = 8
LINE_BYTES = 16
RUN = 4


def tile_picked_recnn_tanh_po_kernel(
    tc, x_words, x_scales, w1_words, w1_scales, gn, w2_words, w2_scales, w3_words, w3_scales,
    res, w4_words, w4_scales, offs, lc, rc, out_0, out_1, out_2,
):
    nc = tc.nc

    with ExitStack() as ctx:
        lists = ctx.enter_context(tc.tile_pool(name="lists", bufs=1))
        keep = ctx.enter_context(tc.tile_pool(name="keep", bufs=1))
        reused = ctx.enter_context(tc.tile_pool(name="reused", bufs=1))
        per_block = ctx.enter_context(tc.tile_pool(name="per_block", bufs=BLOCKS))
        psum = ctx.enter_context(tc.psum_pool(name="psum", bufs=8))

        def load_words(tile, words):
            nc.sync.dma_start(out=tile[:].bitcast(I32), in_=words[0].bitcast(I32))

        def load_scale_rows(tile, first, scales):
            for q in range(QUADRANTS):
                rows = tile[32 * q + first : 32 * q + first + 4, :]
                nc.sync.dma_start(out=rows.bitcast(I32), in_=scales[0, 4 * q : 4 * q + 4, :].bitcast(I32))

        def deal_words(raw, dealt, first=0, last=PACK):
            steps = P // LINE_WORDS
            nc.vector.tensor_copy(
                out=dealt[:].bitcast(U16).rearrange("p (t s m) -> p s t m", s=steps, m=LINE_WORDS),
                in_=raw[:].bitcast(U16).rearrange("p (s m t) -> p s t m", s=steps, t=PACK)[:, :, first:last],
            )
            return dealt

        def deal_scales(raw, dealt):
            steps = P // LINE_BYTES
            nc.vector.tensor_copy(
                out=dealt[:].rearrange("p (t s m) -> p s t m", s=steps, m=LINE_BYTES),
                in_=raw[:].rearrange("p (s m t) -> p s t m", s=steps, t=PACK),
            )
            return dealt

        def product(out, weight, place, codes, scales, start, stop):
            dealt_words, dealt_scales = weight
            nc.tensor.matmul_mx(
                out=out,
                lhsT=dealt_words[:, 2 * P * place : 2 * P * (place + 1)].bitcast(FP4X4),
                lhsT_scale=dealt_scales[:, P * place : P * (place + 1)],
                rhs=codes.bitcast(FP8X4),
                rhs_scale=scales,
                start=start,
                stop=stop,
            )

        def regroup(b, grouped, tiles):
            copy = nc.vector.tensor_copy if b == BLOCKS - 1 else nc.scalar.copy
            copy(
                out=grouped.rearrange("p (c i) t -> p c t i", i=RUN),
                in_=tiles.rearrange("p t (c i) -> p c t i", i=RUN),
            )

        def quantise(codes, scales, grouped):
            nc.vector.quantize_mx(out=codes.bitcast(FP8X4), scales=scales, in_=grouped.rearrange("p v t -> p (v t)"))

        def bank():
            return psum.tile([P, BANK], F32, name="bank")

        def bank_of_tiles():
            return bank()[:].rearrange("p (t v) -> p t v", t=PACK)

        offs_sb = lists.tile([P, S // PER_COL], U16, name="offs_sb")
        lc_sb = lists.tile([P, V // PER_COL], U16, name="lc_sb")
        rc_sb = lists.tile([P, V // PER_COL], U16, name="rc_sb")
        token_scales = keep.tile([P, T], U8, name="token_scales", align_bytes=64)
        token_words = reused.tile([P, T], U32, name="token_words", offset=0, align_bytes=64)
        w1_rows = keep.tile([P, H], U8, name="w1_rows", tag="w1_rows", align_bytes=64)
        packed_rows = keep.tile([P, H], U8, name="packed_rows", align_bytes=64)
        moved_rows = keep.tile([P, 2 * H], U8, name="moved_rows", align_bytes=64)
        w1_raw, w2_raw, w3_raw, w4_raw = [
            keep.tile([P, WORD_BYTES], U8, name="w%d_raw" % j, align_bytes=64) for j in (1, 2, 3, 4)
        ]
        gain = keep.tile([P, PACK], F32, name="gain")
        res_sb = keep.tile([P, PACK, V], F32, name="res_sb", align_bytes=64)

        for tile in (token_scales, w1_rows, packed_rows, moved_rows):
            nc.vector.memset(tile[:].bitcast(I32), 0)
        nc.gpsimd.dma_start(out=gain[:], in_=gn.rearrange("(p t) o -> p (t o)", t=PACK))
        nc.sync.dma_start(offs_sb[:], offs)
        load_scale_rows(token_scales, 0, x_scales)
        nc.sync.dma_start(lc_sb[:], lc)
        nc.sync.dma_start(rc_sb[:], rc)
        nc.sync.dma_start(out=token_words[:].bitcast(I32), in_=x_words[0].rearrange("p n t -> p (n t)").bitcast(I32))
        load_words(w1_raw, w1_words)
        load_scale_rows(w1_rows, 0, w1_scales)
        load_words(w2_raw, w2_words)
        load_words(w3_raw, w3_words)
        for j, scales in enumerate((w2_scales, w3_scales, w4_scales)):
            load_scale_rows(packed_rows, 4 * j, scales)
        load_words(w4_raw, w4_words)
        nc.sync.dma_start(out=res_sb[:], in_=res.rearrange("(p t) v -> p t v", t=PACK))

        leaf_words = [keep.tile([P, LEAVES], U32, name="leaf_words0", align_bytes=64)]
        leaf_scales = [keep.tile([P, LEAVES], U8, name="leaf_scales%d" % half, align_bytes=64) for half in range(2)]

        def pick(half, picked, window):
            columns = LEAVES // PER_COL
            entries = offs_sb[:, columns * half : columns * (half + 1)]
            nc.vector.tensor_copy(out=picked[:], in_=window[:].indirect(entries))

        def after_tokens(name, size, place):
            return reused.tile([P, size], U8, name=name, offset=WORD_BYTES * place, align_bytes=64)

        pick(0, leaf_scales[0], token_scales)
        pick(1, leaf_scales[1], token_scales)
        pick(0, leaf_words[0], token_words)
        first_words = deal_words(w1_raw, keep.tile([P, 2 * P], U8, name="first_words", align_bytes=64), 0, 1)
        w1_plane = deal_scales(w1_rows, keep.tile([P, H], U8, name="w1_plane", align_bytes=64))
        leaf_words.append(keep.tile([P, LEAVES], U32, name="leaf_words1", tag="w1_rows", align_bytes=64))
        pick(1, leaf_words[1], token_words)
        rest_words = deal_words(w1_raw, after_tokens("rest_words", 2 * P * (PACK - 1), 0), 1, PACK)
        w1_first = (first_words, w1_plane[:, 0:P])
        w1_rest = (rest_words, w1_plane[:, P:H])
        w2_dealt = deal_words(w2_raw, after_tokens("w2_dealt", WORD_BYTES, 1))
        w3_dealt = deal_words(w3_raw, after_tokens("w3_dealt", WORD_BYTES, 2))
        packed_plane = deal_scales(packed_rows, after_tokens("packed_plane", H, 4))

        windows = [keep.tile([P, S], F32, name="window%d" % t, align_bytes=64) for t in range(PACK)]

        def project(half, t):
            acc = bank()
            weight, place = (w1_first, 0) if t == 0 else (w1_rest, t - 1)
            product(acc[:], weight, place, leaf_words[half][:], leaf_scales[half][:], True, True)
            h = keep.tile([P, LEAVES], F32, name="h%d%d" % (half, t), align_bytes=64)
            nc.scalar.activation(out=h[:], in_=acc[:], func=TANH)
            gained = windows[t][:, LEAVES * half : LEAVES * (half + 1)]
            if t == 0:
                nc.vector.tensor_scalar(out=gained, in0=h[:], scalar1=gain[:, t : t + 1], scalar2=None, op0=MULT)
            else:
                nc.scalar.activation(out=gained, in_=h[:], func=COPY, scale=gain[:, t : t + 1])

        def children(name, tag):
            return keep.tile([P, PACK, CHUNK], BF16, name=name, tag=tag, align_bytes=64)

        def fetch(fetched, list_sb, c, t):
            columns = CHUNK // PER_COL
            entries = list_sb[:, columns * c : columns * (c + 1)]
            nc.vector.tensor_copy(out=fetched[:, t, :], in_=windows[t][:].indirect(entries))

        left0 = children("left0", "left0")
        right0 = children("right0", "right0")
        for t in range(PACK):
            project(0, t)
            project(1, t)
            fetch(left0, lc_sb, 0, t)
            fetch(right0, rc_sb, 0, t)
        for j in (1, 2):
            for q in range(QUADRANTS):
                nc.sync.dma_start(
                    out=moved_rows[32 * q : 32 * q + 4, H * (j - 1) : H * j].bitcast(I32),
                    in_=packed_plane[32 * q + 4 * j : 32 * q + 4 * j + 4, :].bitcast(I32),
                )
        w2 = (w2_dealt, packed_plane[:])
        w3 = (w3_dealt, moved_rows[:, 0:H])

        y_words = keep.tile([P, V], U32, name="y_words", align_bytes=64)
        y_scales = keep.tile([P, V], U8, name="y_scales", align_bytes=64)
        y_chunks = [keep.tile([P, PACK, CHUNK], F32, name="y%d" % c, align_bytes=64) for c in range(V // CHUNK)]
        out_rows = out_0.rearrange("(p t) v -> p t v", t=PACK)
        out_words = out_1[0].rearrange("p v t -> p (v t)").bitcast(I32)

        def mx_operand(name, width):
            codes = keep.tile([P, width], U32, name=name + "_codes", tag=name + "_codes", align_bytes=64)
            scales = keep.tile([P, width], U8, name=name + "_scales", tag=name + "_scales", align_bytes=64)
            return codes, scales

        def quantise_left(c, fetched):
            grouped = keep.tile([P, CHUNK, PACK], BF16, name="zl%d_grouped" % c, align_bytes=64)
            regroup(PER_CHUNK * c, grouped[:], fetched[:])
            codes, scales = mx_operand("zl%d" % c, CHUNK)
            quantise(codes[:], scales[:], grouped[:])
            return codes, scales

        zr_grouped_tags = ("zr0_grouped", "zr1_grouped", "zr0_codes", "zr0_scales")

        def combine(b, zl, fetched):
            inner = slice(BLOCK * (b % PER_CHUNK), BLOCK * (b % PER_CHUNK + 1))
            grouped = keep.tile([P, BLOCK, PACK], BF16, name="zr%d_grouped" % b, tag=zr_grouped_tags[b], align_bytes=64)
            regroup(b, grouped[:], fetched[:, :, inner])
            codes, scales = mx_operand("zr%d" % b, BLOCK)
            quantise(codes[:], scales[:], grouped[:])
            acc = bank_of_tiles()
            for t in range(PACK):
                product(acc[:, t, :], w2, t, zl[0][:, inner], zl[1][:, inner], True, False)
                product(acc[:, t, :], w3, t, codes[:], scales[:], False, True)
            return acc

        def squash(acc):
            state = per_block.tile([P, BLOCK, PACK], F32, name="state", align_bytes=64)
            nc.scalar.activation(out=state[:], in_=acc.rearrange("p t v -> p v t"), func=TANH)
            return state

        def apply_gain(state):
            z = per_block.tile([P, BLOCK, PACK], BF16, name="z", align_bytes=64)
            gains = gain[:].unsqueeze(1).to_broadcast([P, BLOCK, PACK])
            nc.vector.tensor_tensor(out=z[:], in0=state[:], in1=gains, op=MULT)
            return z

        def output_layer(z):
            z_codes = per_block.tile([P, BLOCK], U32, name="z_codes", align_bytes=64)
            z_scales = per_block.tile([P, BLOCK], U8, name="z_scales", align_bytes=64)
            quantise(z_codes[:], z_scales[:], z[:])
            acc = bank_of_tiles()
            for t in range(PACK):
                product(acc[:, t, :], w4, t, z_codes[:], z_scales[:], True, True)
            return acc

        def add_residual(b, acc):
            c, j = divmod(b, PER_CHUNK)
            y = y_chunks[c][:, :, BLOCK * j : BLOCK * (j + 1)]
            nc.vector.tensor_tensor(out=y, in0=acc, in1=res_sb[:, :, BLOCK * b : BLOCK * (b + 1)], op=ADD)
            if j == PER_CHUNK - 1:
                nc.sync.dma_start(out=out_rows[:, :, CHUNK * c : CHUNK * (c + 1)], in_=y_chunks[c][:])
            return y

        def hand_on(b, y):
            c, j = divmod(b, PER_CHUNK)
            nodes = slice(BLOCK * b, BLOCK * (b + 1))
            y_grouped = per_block.tile([P, BLOCK, PACK], BF16, name="y_grouped", align_bytes=64)
            regroup(b, y_grouped[:], y)
            quantise(y_words[:, nodes], y_scales[:, nodes], y_grouped[:])
            if j == PER_CHUNK - 1:
                chunk = slice(CHUNK * c, CHUNK * (c + 1))
                nc.sync.dma_start(out=out_words[:, chunk], in_=y_words[:, chunk].bitcast(I32))

        zl0 = quantise_left(0, left0)
        accs = [combine(b, zl0, right0) for b in range(PER_CHUNK)]
        left1 = children("left1", "left1")
        right1 = children("right1", "left0")
        for t in range(PACK):
            fetch(left1, lc_sb, 1, t)
        for t in range(PACK):
            fetch(right1, rc_sb, 1, t)
        zl1 = quantise_left(1, left1)
        states = [squash(acc) for acc in accs]
        accs = [combine(b, zl1, right1) for b in range(PER_CHUNK, BLOCKS)]
        states.extend([squash(acc) for acc in accs])
        w4 = (deal_words(w4_raw, after_tokens("w4_dealt", WORD_BYTES, 3)), moved_rows[:, H : 2 * H])

        zs = [apply_gain(states[0])]
        out_accs = []
        for b in range(BLOCKS):
            if b + 1 < BLOCKS:
                zs.append(apply_gain(states[b + 1]))
            out_accs.append(output_layer(zs[b]))
        ys = [add_residual(b, acc) for b, acc in enumerate(out_accs)]
        for b, y in enumerate(ys):
            hand_on(b, y)

        for q in range(QUADRANTS):
            queue = (nc.scalar, nc.sync)[q % 2]
            queue.dma_start(
                out=out_2[0, 4 * q : 4 * q + 4, :].bitcast(I32), in_=y_scales[32 * q : 32 * q + 4, :].bitcast(I32)
            )
